import numpy as np
import ml_dtypes


def mxq(x, axis, fmt="e4m3"):
    dtype, down = {"e4m3": (ml_dtypes.float8_e4m3fn, 7), "e5m2": (ml_dtypes.float8_e5m2, 14)}[fmt]
    v = np.moveaxis(np.asarray(x, np.float32).astype(ml_dtypes.bfloat16).astype(np.float64), axis, -1)
    blocks = v.reshape(v.shape[:-1] + (-1, 32))
    amax = np.abs(blocks).max(-1, keepdims=True)
    byte = np.maximum(np.where(amax > 0, np.frexp(amax)[1] - 1 + 127, 0) - down, 1)
    scale = np.exp2(byte - 127.0)
    codes = (blocks / scale).astype(np.float32).astype(dtype).astype(np.float64)
    return np.moveaxis((codes * scale).reshape(v.shape), -1, axis)


WIDE = False


def mx_kscale(k):
    if not WIDE:
        return np.ones(k)
    levels = np.array([30, -30])
    if k % 512:
        return np.exp2(np.random.permutation(np.resize(levels, k // 32))).repeat(32)
    a = np.empty((k // 512, 16))
    for p in range(k // 512):
        a[p, :8] = np.random.permutation(np.resize(levels, 8))
        for g in range(8):
            far = levels[np.abs(levels - a[p, g]) >= 10]
            a[p, g + 8] = far[np.random.randint(len(far))]
    return np.exp2(a.ravel()).repeat(32)


BF16 = ml_dtypes.bfloat16


def bf(x):
    return np.asarray(x, np.float32).astype(BF16)


def f64(x):
    return np.asarray(x).astype(np.float64)


E2M1 = np.array([0.0, 0.5, 1.0, 1.5, 2.0, 3.0, 4.0, 6.0, -0.0, -0.5, -1.0, -1.5, -2.0, -3.0, -4.0, -6.0])


def pack_weight(w, fmt):
    k, n = w.shape
    w = f64(bf(w)).reshape(k // 32, 32, n)
    amax = np.abs(w).max(1)
    if fmt == "e4m3":
        byte = np.frexp(amax)[1] - 1 + 127 - 7
    else:
        mant, ex = np.frexp(amax / 6.0)
        byte = np.where(mant > 0.5, ex, ex - 1) + 127
    byte = np.clip(np.where(amax > 0, byte, 1), 1, 254)
    scaled = (w * np.exp2(127.0 - byte)[:, None, :]).reshape(k, n).astype(np.float32)
    by_word = np.ascontiguousarray(scaled.reshape(k // 512, 128, 4, n).transpose(0, 1, 3, 2))
    if fmt == "e4m3":
        words = by_word.astype(ml_dtypes.float8_e4m3fn).view(np.uint8)
    else:
        c = by_word.astype(ml_dtypes.float4_e2m1fn).view(np.uint8) & 0xF
        words = c[..., 0::2] | (c[..., 1::2] << 4)
    return np.ascontiguousarray(words), np.ascontiguousarray(byte.astype(np.uint8).reshape(k // 512, 16, n))


def unpack_weight(words, scales, fmt):
    g, p, n, _ = words.shape
    if fmt == "e4m3":
        vals = np.ascontiguousarray(words).view(ml_dtypes.float8_e4m3fn).astype(np.float64)
    else:
        nib = np.empty((g, p, n, 4), np.uint8)
        nib[..., 0::2] = words & 0xF
        nib[..., 1::2] = words >> 4
        vals = E2M1[nib]
    vals = vals * np.repeat(np.exp2(scales.astype(np.float64) - 127.0), 8, axis=1)[..., None]
    return vals.transpose(0, 1, 3, 2).reshape(g * 512, n)
def pack4(w):
    words, scales = pack_weight(w, "e2m1")
    return words.reshape(words.shape[0], 128, -1), scales


def unpack4(words, scales):
    return unpack_weight(words.reshape(words.shape[0], 128, -1, 2), scales, "e2m1")


NB, NM, NY, G = 2, 512, 512, 1536


def setup_inputs():
    s = mx_kscale(G)
    t = mx_kscale(G)
    a = np.random.standard_normal((G, G))
    eta = (a + a.T) / np.sqrt(2.0) / np.sqrt(G)
    eta_words, eta_scales = pack4(eta / s[:, None] * t)
    return {"x": bf(np.random.standard_normal((NB, NM, G)) * s),
            "kappa": bf(np.random.uniform(0.5, 1.5, (NB, G))),
            "eta_words": eta_words,
            "eta_scales": eta_scales,
            "y": bf(np.random.standard_normal((NB, NY, G)) / np.sqrt(G) / t)}


def reference(x, kappa, eta_words, eta_scales, y):
    eta = unpack4(eta_words, eta_scales)
    mag = f64(kappa)[:, None, :]
    v = f64(x) * mag
    vq = mxq(v, 2, "e4m3")
    u = vq.reshape(NB * NM, G) @ eta
    z = u.reshape(NB, NM, G) * mag
    zq = mxq(z, 2, "e5m2")
    yq = mxq(f64(y), 2, "e4m3")
    return zq @ yq.swapaxes(1, 2)

@@ -1,0 +1,322 @@
+from contextlib import ExitStack
+
+import concourse.mybir as mybir
+from concourse.masks import make_identity
+
+NB, NM, NY, G = 2, 512, 512, 1536
+P = 128
+K_PASS = 512
+NH = G // K_PASS
+PACK = 4
+
+F32 = mybir.dt.float32
+BF16 = mybir.dt.bfloat16
+I32 = mybir.dt.int32
+U32 = mybir.dt.uint32
+U8 = mybir.dt.uint8
+E4M3 = mybir.dt.float8_e4m3fn_x4
+E5M2 = mybir.dt.float8_e5m2_x4
+E2M1 = mybir.dt.float4_e2m1fn_x4
+MULT = mybir.AluOpType.mult
+COPY = mybir.ActivationFunctionType.Copy
+
+FLOPS = 2 * NB * NM * G * (G + NY)
+
+
+def tile_photonic_rayleigh_gram_s9_kernel(tc, x, kappa, eta_words, eta_scales, y, out):
+    nc = tc.nc
+    with ExitStack() as ctx:
+        ctx.enter_context(tc.manual_schedule())
+        keep = ctx.enter_context(tc.tile_pool(name="keep", bufs=1))
+        work = ctx.enter_context(tc.tile_pool(name="work", bufs=2))
+        psum = ctx.enter_context(tc.psum_pool(name="psum", bufs=4))
+
+        def kept(name, shape, dtype):
+            return keep.tile(shape, dtype, name=name, tag=name, align_bytes=64)
+
+        def worked(name, shape, dtype, bufs):
+            return work.tile(shape, dtype, name=name, tag=name, bufs=bufs, align_bytes=64)
+
+        def bank(tag, shape, dtype):
+            return psum.tile(shape, dtype, name="bank_" + tag, tag=tag, bufs=4)
+
+        x_raw = [[kept("x_raw%d%d" % (b, q), [P, 2, G], BF16) for q in range(2)] for b in range(NB)]
+        y_raw = [[kept("y_raw%d%d" % (b, q), [P, 2, G], BF16) for q in range(2)] for b in range(NB)]
+        eta_raw = [kept("eta_raw%d" % h, [P, NH, 2 * K_PASS], U8) for h in range(NH)]
+        scl_raw = kept("scl_raw", [P, NH, G], U8)
+        kap_rows = kept("kap_rows", [P, K_PASS], BF16)
+
+        nc.vector.memset(kap_rows[:], 0.0)
+        nc.vector.memset(scl_raw[:].rearrange("p g n -> p (g n)").bitcast(I32), 0)
+        ident_b = kept("ident_b", [P, P], BF16)
+        ident_f = kept("ident_f", [P, P], F32)
+        make_identity(nc, ident_b[:])
+        make_identity(nc, ident_f[:])
+
+        def rows_of(src, b, q):
+            return src[b, 2 * P * q : 2 * P * (q + 1), :].rearrange("(a p) k -> p a k", p=P)
+
+        def load_eta(h):
+            nc.sync.dma_start(
+                out=eta_raw[h][:],
+                in_=eta_words[:, :, 2 * K_PASS * h : 2 * K_PASS * (h + 1)].rearrange("g p n -> p g n"),
+            )
+
+        nc.sync.dma_start(out=x_raw[0][0][:, :, 0:K_PASS], in_=rows_of(x, 0, 0)[:, :, 0:K_PASS])
+        nc.sync.dma_start(out=kap_rows[0 : NB * NH, :], in_=kappa.rearrange("b (h k) -> (b h) k", h=NH))
+        for q in range(2):
+            for g in range(NH):
+                if q + g > 0:
+                    cols = slice(g * K_PASS, (g + 1) * K_PASS)
+                    nc.sync.dma_start(out=x_raw[0][q][:, :, cols], in_=rows_of(x, 0, q)[:, :, cols])
+        for quad in range(4):
+            nc.sync.dma_start(
+                out=scl_raw[32 * quad : 32 * quad + 4, :, :].bitcast(I32),
+                in_=eta_scales[:, 4 * quad : 4 * quad + 4, :].rearrange("g r n -> r g n").bitcast(I32),
+            )
+        load_eta(0)
+        nc.sync.dma_start(out=x_raw[1][0][:], in_=rows_of(x, 1, 0))
+        nc.sync.dma_start(out=x_raw[1][1][:], in_=rows_of(x, 1, 1))
+        load_eta(1)
+        nc.sync.dma_start(out=y_raw[0][0][:], in_=rows_of(y, 0, 0))
+        load_eta(2)
+        nc.sync.dma_start(out=y_raw[0][1][:], in_=rows_of(y, 0, 1))
+        nc.sync.dma_start(out=y_raw[1][0][:], in_=rows_of(y, 1, 0))
+        nc.sync.dma_start(out=y_raw[1][1][:], in_=rows_of(y, 1, 1))
+
+        kap_perm = kept("kap_perm", [P, K_PASS], BF16)
+        nc.vector.tensor_copy(
+            out=kap_perm[:].rearrange("p (t b m) -> p t b m", t=4, m=8),
+            in_=kap_rows[:].rearrange("p (b t m) -> p t b m", t=4, m=8),
+        )
+        kap_bank = bank("acc", [P, 8, P], BF16)
+        for t in range(PACK):
+            nc.tensor.transpose(kap_bank[:, t, :], kap_rows[:, t::PACK], ident_b[:])
+            nc.tensor.transpose(kap_bank[:, 4 + t, :], kap_perm[:, t * P : (t + 1) * P], ident_b[:])
+        kap_x = kept("kap_x", [P, NB * NH, PACK], BF16)
+        kap_z = kept("kap_z", [P, PACK, NB * NH], F32)
+        nc.scalar.copy(out=kap_x[:], in_=kap_bank[:, 0:4, 0 : NB * NH].rearrange("p t b -> p b t"))
+        nc.scalar.copy(out=kap_z[:], in_=kap_bank[:, 4:8, 0 : NB * NH])
+
+        v_codes = [kept("v_codes%d" % b, [P, NH, NM], U32) for b in range(NB)]
+        v_scl = [kept("v_scl%d" % b, [P, NH, NM], U8) for b in range(NB)]
+        y_codes = [kept("y_codes%d" % b, [P, NH, NY], U32) for b in range(NB)]
+        y_scl = [kept("y_scl%d" % b, [P, NH, NY], U8) for b in range(NB)]
+        z_codes = [[kept("z_codes%d%d" % (b, h), [P, NM], U32) for h in range(NH)] for b in range(NB)]
+        z_scl = [[kept("z_scl%d%d" % (b, h), [P, NM], U8) for h in range(NH)] for b in range(NB)]
+        eta_st = [kept("eta_st%d" % h, [P, PACK, NH, 2 * P], U8) for h in range(NH)]
+        scl_st = kept("scl_st", [P, PACK, NH, NH, P], U8)
+
+        def permute_eta(h):
+            nc.vector.tensor_copy(
+                out=eta_st[h][:].rearrange("p t g n -> p (t g n)").bitcast(I32).rearrange("p (t b w) -> p t b w", t=4, w=4),
+                in_=eta_raw[h][:].rearrange("p g n -> p (g n)").bitcast(I32).rearrange("p (b t w) -> p t b w", t=4, w=4),
+            )
+
+        def permute_scales():
+            nc.vector.tensor_copy(
+                out=scl_st[:].rearrange("p t g h n -> p (t g h n)").bitcast(I32).rearrange("p (t b w) -> p t b w", t=4, w=2),
+                in_=scl_raw[:].rearrange("p g n -> p (g n)").bitcast(I32).rearrange("p (b t w) -> p t b w", t=4, w=2),
+            )
+
+        def turn_x(b, q, g, tag):
+            turned = bank(tag, [P, 2, 2 * P], F32)
+            for a in range(2):
+                words = x_raw[b][q][:, a, :].bitcast(F32)
+                for u in range(2):
+                    nc.tensor.transpose(turned[:, u, a * P : (a + 1) * P], words[:, 256 * g + u : 256 * (g + 1) : 2], ident_f[:])
+            return turned
+
+        def kap_for(b, g):
+            row = kap_x[:, b * NH + g, :].unsqueeze(1).to_broadcast([P, 2 * P, PACK])
+            return row
+
+        def scale_x_psum(b, g, turned):
+            v = worked("v", [P, 2 * P, PACK], BF16, 4)
+            nc.vector.tensor_tensor(
+                out=v[:].rearrange("p r (u e) -> p r u e", e=2),
+                in0=turned[:].rearrange("p u r -> p (u r)").bitcast(BF16).rearrange("p (u r e) -> p r u e", u=2, e=2),
+                in1=kap_for(b, g).rearrange("p r (u e) -> p r u e", e=2),
+                op=MULT,
+            )
+            return v
+
+        def fetch_x(turned):
+            xt = worked("xt", [P, 2 * P, PACK], BF16, 6)
+            nc.scalar.copy(
+                out=xt[:].rearrange("p r t -> p (r t)").bitcast(F32).rearrange("p (r u) -> p r u", u=2),
+                in_=turned[:].rearrange("p u r -> p r u"),
+            )
+            return xt
+
+        def scale_x(b, g, xt):
+            v = worked("v", [P, 2 * P, PACK], BF16, 4)
+            nc.vector.tensor_tensor(out=v[:], in0=xt[:], in1=kap_for(b, g), op=MULT)
+            return v
+
+        def quant_x(b, q, g, v):
+            cols = slice(2 * P * q, 2 * P * (q + 1))
+            nc.vector.quantize_mx(
+                out=v_codes[b][:, g, cols].bitcast(E4M3), scales=v_scl[b][:, g, cols], in_=v[:].rearrange("p r t -> p (r t)")
+            )
+
+        def reorder_y(b, q):
+            yo = worked("yo", [P, 2, PACK, G // PACK], BF16, 2)
+            for a in range(2):
+                nc.vector.tensor_copy(
+                    out=yo[:, a, :, :].rearrange("p t (b m) -> p t b m", m=8),
+                    in_=y_raw[b][q][:, a, :].rearrange("p (b t m) -> p t b m", t=4, m=8),
+                )
+            return yo
+
+        def turn_y(yo):
+            fetched = []
+            for h in range(NH):
+                turned = bank("tr", [P, PACK, 2 * P], BF16)
+                for a in range(2):
+                    for t in range(PACK):
+                        nc.tensor.transpose(turned[:, t, a * P : (a + 1) * P], yo[:, a, t, h * P : (h + 1) * P], ident_b[:])
+                yt = worked("yt", [P, 2 * P, PACK], BF16, 6)
+                nc.scalar.copy(out=yt[:], in_=turned[:].rearrange("p t r -> p r t"))
+                fetched.append(yt)
+            return fetched
+
+        def quant_y(b, q, fetched):
+            cols = slice(2 * P * q, 2 * P * (q + 1))
+            for h in range(NH):
+                nc.vector.quantize_mx(
+                    out=y_codes[b][:, h, cols].bitcast(E4M3),
+                    scales=y_scl[b][:, h, cols],
+                    in_=fetched[h][:].rearrange("p r t -> p (r t)"),
+                )
+
+        def stage1(b, h):
+            zs = worked("zs", [P, PACK, NM], BF16, 2)
+            for t in range(PACK):
+                acc = bank("acc", [P, NM], F32)
+                for g in range(NH):
+                    nc.tensor.matmul_mx(
+                        out=acc[:],
+                        lhsT=eta_st[h][:, t, g, :].bitcast(E2M1),
+                        lhsT_scale=scl_st[:, t, g, h, :],
+                        rhs=v_codes[b][:, g, :].bitcast(E4M3),
+                        rhs_scale=v_scl[b][:, g, :],
+                        start=(g == 0),
+                        stop=(g == NH - 1),
+                    )
+                col = b * NH + h
+                nc.scalar.activation(out=zs[:, t, :], in_=acc[:], func=COPY, scale=kap_z[:, t, col : col + 1])
+            return zs
+
+        def pack_z(zs):
+            zi = worked("zi", [P, NM, PACK], BF16, 2)
+            nc.vector.tensor_copy(out=zi[:], in_=zs[:].rearrange("p t n -> p n t"))
+            return zi
+
+        def quant_z(b, h, zi):
+            nc.vector.quantize_mx(
+                out=z_codes[b][h][:].bitcast(E5M2), scales=z_scl[b][h][:], in_=zi[:].rearrange("p n t -> p (n t)")
+            )
+
+        def project(b, i, acc, hs):
+            for h in hs:
+                nc.tensor.matmul_mx(
+                    out=acc[:],
+                    lhsT=z_codes[b][h][:, i * P : (i + 1) * P].bitcast(E5M2),
+                    lhsT_scale=z_scl[b][h][:, i * P : (i + 1) * P],
+                    rhs=y_codes[b][:, h, :].bitcast(E4M3),
+                    rhs_scale=y_scl[b][:, h, :],
+                    start=(h == 0),
+                    stop=(h == NH - 1),
+                )
+
+        def store(b, i, acc, on_vector):
+            res = worked("res", [P, NY], F32, 8)
+            if on_vector:
+                nc.vector.tensor_copy(out=res[:], in_=acc[:])
+            else:
+                nc.scalar.copy(out=res[:], in_=acc[:])
+            nc.sync.dma_start(out=out[b, i * P : (i + 1) * P, :], in_=res[:])
+
+        units = [(q, g) for q in range(2) for g in range(NH)]
+        t0 = [turn_x(0, q, g, "tr") for q, g in units[:4]]
+        v0 = [scale_x_psum(0, units[0][1], t0[0])]
+        for n in range(1, 6):
+            if n + 3 < 6:
+                q, g = units[n + 3]
+                t0.append(turn_x(0, q, g, "tr"))
+            v0.append(scale_x_psum(0, units[n][1], t0[n]))
+            quant_x(0, units[n - 1][0], units[n - 1][1], v0[n - 1])
+            if n == 3:
+                permute_scales()
+            if n == 4:
+                permute_eta(0)
+        quant_x(0, units[5][0], units[5][1], v0[5])
+        xt1 = []
+        for n in range(6):
+            q, g = units[n]
+            xt1.append(fetch_x(turn_x(1, q, g, "acc" if n < 4 else "tr")))
+
+        pending = []
+
+        def x1_step(n):
+            pending.append((n, scale_x(1, units[n][1], xt1[n])))
+            if len(pending) > 1:
+                x1_quant()
+
+        def x1_quant():
+            n, v = pending.pop(0)
+            quant_x(1, units[n][0], units[n][1], v)
+
+        permute_eta(1)
+        zs00 = stage1(0, 0)
+        x1_step(0)
+        x1_step(1)
+        yo00 = reorder_y(0, 0)
+        zs01 = stage1(0, 1)
+        zi00 = pack_z(zs00)
+        x1_step(2)
+        quant_z(0, 0, zi00)
+        x1_step(3)
+        permute_eta(2)
+        yt00 = turn_y(yo00)
+        zs02 = stage1(0, 2)
+        zi01 = pack_z(zs01)
+        x1_step(4)
+        quant_z(0, 1, zi01)
+        x1_step(5)
+        x1_quant()
+        yo01 = reorder_y(0, 1)
+        quant_y(0, 0, yt00)
+        yt01 = turn_y(yo01)
+        zs10 = stage1(1, 0)
+        zi02 = pack_z(zs02)
+        yo10 = reorder_y(1, 0)
+        quant_z(0, 2, zi02)
+        quant_y(0, 1, yt01)
+        yt10 = turn_y(yo10)
+        zs11 = stage1(1, 1)
+        zi10 = pack_z(zs10)
+        yo11 = reorder_y(1, 1)
+        quant_z(1, 0, zi10)
+        quant_y(1, 0, yt10)
+        yt11 = turn_y(yo11)
+        zs12 = stage1(1, 2)
+        zi11 = pack_z(zs11)
+        quant_y(1, 1, yt11)
+        quant_z(1, 1, zi11)
+
+        for i in range(NM // P):
+            acc = bank("tr", [P, NY], F32)
+            project(0, i, acc, range(NH))
+            store(0, i, acc, False)
+        zi12 = pack_z(zs12)
+        quant_z(1, 2, zi12)
+        accs = []
+        for i in range(NM // P):
+            acc = bank("acc", [P, NY], F32)
+            project(1, i, acc, range(NH - 1))
+            accs.append(acc)
+        for i in range(NM // P):
+            project(1, i, accs[i], [NH - 1])
+            store(1, i, accs[i], i % 2 == 1)

@@ -40,14 +40,14 @@ def tile_photonic_rayleigh_gram_s9_kernel(tc, x, kappa, eta_words, eta_scales, y
         def bank(tag, shape, dtype):
             return psum.tile(shape, dtype, name="bank_" + tag, tag=tag, bufs=4)
 
-        x_raw = [[kept("x_raw%d%d" % (b, q), [P, 2, G], BF16) for q in range(2)] for b in range(NB)]
+        x_raw = [kept("x_raw%d" % b, [P, NM // P, G], BF16) for b in range(NB)]
         y_raw = [[kept("y_raw%d%d" % (b, q), [P, 2, G], BF16) for q in range(2)] for b in range(NB)]
         eta_raw = [kept("eta_raw%d" % h, [P, NH, 2 * K_PASS], U8) for h in range(NH)]
         scl_raw = kept("scl_raw", [P, NH, G], U8)
         kap_rows = kept("kap_rows", [P, K_PASS], BF16)
 
-        nc.vector.memset(kap_rows[:], 0.0)
         nc.vector.memset(scl_raw[:].rearrange("p g n -> p (g n)").bitcast(I32), 0)
+        nc.gpsimd.memset(kap_rows[:], 0.0)
         ident_b = kept("ident_b", [P, P], BF16)
         ident_f = kept("ident_f", [P, P], F32)
         make_identity(nc, ident_b[:])
@@ -62,21 +62,25 @@ def tile_photonic_rayleigh_gram_s9_kernel(tc, x, kappa, eta_words, eta_scales, y
                 in_=eta_words[:, :, 2 * K_PASS * h : 2 * K_PASS * (h + 1)].rearrange("g p n -> p g n"),
             )
 
-        nc.sync.dma_start(out=x_raw[0][0][:, :, 0:K_PASS], in_=rows_of(x, 0, 0)[:, :, 0:K_PASS])
-        nc.sync.dma_start(out=kap_rows[0 : NB * NH, :], in_=kappa.rearrange("b (h k) -> (b h) k", h=NH))
-        for q in range(2):
-            for g in range(NH):
-                if q + g > 0:
-                    cols = slice(g * K_PASS, (g + 1) * K_PASS)
-                    nc.sync.dma_start(out=x_raw[0][q][:, :, cols], in_=rows_of(x, 0, q)[:, :, cols])
-        for quad in range(4):
+        def load_x(b, a0, a1, g0, g1):
             nc.sync.dma_start(
+                out=x_raw[b][:, a0:a1, g0 * K_PASS : g1 * K_PASS],
+                in_=x[b, a0 * P : a1 * P, g0 * K_PASS : g1 * K_PASS].rearrange("(a p) k -> p a k", p=P),
+            )
+
+        load_x(0, 0, 2, 0, 1)
+        load_eta(0)
+        load_x(0, 2, 4, 0, 1)
+        nc.scalar.dma_start(out=kap_rows[0 : NB * NH, :], in_=kappa.rearrange("b (h k) -> (b h) k", h=NH))
+        load_x(0, 0, 4, 1, 2)
+        load_x(0, 0, 4, 2, 3)
+        for quad in range(4):
+            nc.scalar.dma_start(
                 out=scl_raw[32 * quad : 32 * quad + 4, :, :].bitcast(I32),
                 in_=eta_scales[:, 4 * quad : 4 * quad + 4, :].rearrange("g r n -> r g n").bitcast(I32),
             )
-        load_eta(0)
-        nc.sync.dma_start(out=x_raw[1][0][:], in_=rows_of(x, 1, 0))
-        nc.sync.dma_start(out=x_raw[1][1][:], in_=rows_of(x, 1, 1))
+        load_x(1, 0, 2, 0, NH)
+        load_x(1, 2, 4, 0, NH)
         load_eta(1)
         nc.sync.dma_start(out=y_raw[0][0][:], in_=rows_of(y, 0, 0))
         load_eta(2)
@@ -89,14 +93,18 @@ def tile_photonic_rayleigh_gram_s9_kernel(tc, x, kappa, eta_words, eta_scales, y
             out=kap_perm[:].rearrange("p (t b m) -> p t b m", t=4, m=8),
             in_=kap_rows[:].rearrange("p (b t m) -> p t b m", t=4, m=8),
         )
-        kap_bank = bank("acc", [P, 8, P], BF16)
-        for t in range(PACK):
-            nc.tensor.transpose(kap_bank[:, t, :], kap_rows[:, t::PACK], ident_b[:])
-            nc.tensor.transpose(kap_bank[:, 4 + t, :], kap_perm[:, t * P : (t + 1) * P], ident_b[:])
         kap_x = kept("kap_x", [P, NB * NH, PACK], BF16)
         kap_z = kept("kap_z", [P, PACK, NB * NH], F32)
-        nc.scalar.copy(out=kap_x[:], in_=kap_bank[:, 0:4, 0 : NB * NH].rearrange("p t b -> p b t"))
-        nc.scalar.copy(out=kap_z[:], in_=kap_bank[:, 4:8, 0 : NB * NH])
+
+        def spread_kappa():
+            kap_bank = bank("acc", [P, 8, P], BF16)
+            for t in range(PACK):
+                nc.tensor.transpose(kap_bank[:, t, :], kap_rows[:, t::PACK], ident_b[:])
+            nc.scalar.copy(out=kap_x[:], in_=kap_bank[:, 0:4, 0 : NB * NH].rearrange("p t b -> p b t"))
+            kap_bank2 = bank("acc", [P, 8, P], BF16)
+            for t in range(PACK):
+                nc.tensor.transpose(kap_bank2[:, t, :], kap_perm[:, t * P : (t + 1) * P], ident_b[:])
+            nc.scalar.copy(out=kap_z[:], in_=kap_bank2[:, 0:4, 0 : NB * NH])
 
         v_codes = [kept("v_codes%d" % b, [P, NH, NM], U32) for b in range(NB)]
         v_scl = [kept("v_scl%d" % b, [P, NH, NM], U8) for b in range(NB)]
@@ -122,7 +130,7 @@ def tile_photonic_rayleigh_gram_s9_kernel(tc, x, kappa, eta_words, eta_scales, y
         def turn_x(b, q, g, tag):
             turned = bank(tag, [P, 2, 2 * P], F32)
             for a in range(2):
-                words = x_raw[b][q][:, a, :].bitcast(F32)
+                words = x_raw[b][:, 2 * q + a, :].bitcast(F32)
                 for u in range(2):
                     nc.tensor.transpose(turned[:, u, a * P : (a + 1) * P], words[:, 256 * g + u : 256 * (g + 1) : 2], ident_f[:])
             return turned
@@ -141,81 +149,83 @@ def tile_photonic_rayleigh_gram_s9_kernel(tc, x, kappa, eta_words, eta_scales, y
             )
             return v
 
-        def fetch_x(turned):
-            xt = worked("xt", [P, 2 * P, PACK], BF16, 6)
-            nc.scalar.copy(
-                out=xt[:].rearrange("p r t -> p (r t)").bitcast(F32).rearrange("p (r u) -> p r u", u=2),
-                in_=turned[:].rearrange("p u r -> p r u"),
-            )
-            return xt
-
-        def scale_x(b, g, xt):
-            v = worked("v", [P, 2 * P, PACK], BF16, 4)
-            nc.vector.tensor_tensor(out=v[:], in0=xt[:], in1=kap_for(b, g), op=MULT)
-            return v
-
         def quant_x(b, q, g, v):
             cols = slice(2 * P * q, 2 * P * (q + 1))
             nc.vector.quantize_mx(
                 out=v_codes[b][:, g, cols].bitcast(E4M3), scales=v_scl[b][:, g, cols], in_=v[:].rearrange("p r t -> p (r t)")
             )
 
-        def reorder_y(b, q):
-            yo = worked("yo", [P, 2, PACK, G // PACK], BF16, 2)
+        yo = {}
+
+        def reorder_y(b, q, a, on_vector):
+            if (b, q) not in yo:
+                yo[b, q] = worked("yo", [P, 2, 2, G // 2], BF16, 4)
+            dst = yo[b, q][:, a, :, :].rearrange("p s (b m e) -> p s b m e", m=8, e=2)
+            src = y_raw[b][q][:, a, :].rearrange("p (b s e m) -> p s b m e", s=2, e=2, m=8)
+            if on_vector:
+                nc.vector.tensor_copy(out=dst, in_=src)
+            else:
+                nc.scalar.copy(out=dst, in_=src)
+
+        yt = {}
+
+        def turn_y(n):
+            b, q, h = n // 6, n // 3 % 2, n % 3
+            turned = bank("tr", [P, 2, 2 * P], F32)
             for a in range(2):
-                nc.vector.tensor_copy(
-                    out=yo[:, a, :, :].rearrange("p t (b m) -> p t b m", m=8),
-                    in_=y_raw[b][q][:, a, :].rearrange("p (b t m) -> p t b m", t=4, m=8),
-                )
-            return yo
+                for s in range(2):
+                    words = yo[b, q][:, a, s, :].bitcast(F32)
+                    nc.tensor.transpose(turned[:, s, a * P : (a + 1) * P], words[:, h * P : (h + 1) * P], ident_f[:])
+            yt[n] = worked("yt", [P, 2 * P, PACK], BF16, 4)
+            nc.scalar.copy(
+                out=yt[n][:].rearrange("p r t -> p (r t)").bitcast(F32).rearrange("p (r s) -> p r s", s=2),
+                in_=turned[:].rearrange("p s r -> p r s"),
+            )
 
-        def turn_y(yo):
-            fetched = []
-            for h in range(NH):
-                turned = bank("tr", [P, PACK, 2 * P], BF16)
-                for a in range(2):
-                    for t in range(PACK):
-                        nc.tensor.transpose(turned[:, t, a * P : (a + 1) * P], yo[:, a, t, h * P : (h + 1) * P], ident_b[:])
-                yt = worked("yt", [P, 2 * P, PACK], BF16, 6)
-                nc.scalar.copy(out=yt[:], in_=turned[:].rearrange("p t r -> p r t"))
-                fetched.append(yt)
-            return fetched
-
-        def quant_y(b, q, fetched):
+        def quant_y(n):
+            b, q, h = n // 6, n // 3 % 2, n % 3
             cols = slice(2 * P * q, 2 * P * (q + 1))
-            for h in range(NH):
-                nc.vector.quantize_mx(
-                    out=y_codes[b][:, h, cols].bitcast(E4M3),
-                    scales=y_scl[b][:, h, cols],
-                    in_=fetched[h][:].rearrange("p r t -> p (r t)"),
-                )
+            nc.vector.quantize_mx(
+                out=y_codes[b][:, h, cols].bitcast(E4M3),
+                scales=y_scl[b][:, h, cols],
+                in_=yt[n][:].rearrange("p r t -> p (r t)"),
+            )
 
-        def stage1(b, h):
-            zs = worked("zs", [P, PACK, NM], BF16, 2)
-            for t in range(PACK):
+        def one_pass(b, h, t, g, acc):
+            nc.tensor.matmul_mx(
+                out=acc[:],
+                lhsT=eta_st[h][:, t, g, :].bitcast(E2M1),
+                lhsT_scale=scl_st[:, t, g, h, :],
+                rhs=v_codes[b][:, g, :].bitcast(E4M3),
+                rhs_scale=v_scl[b][:, g, :],
+                start=(g == 0),
+                stop=(g == NH - 1),
+            )
+
+        zs = {}
+
+        def fetch_z(b, h, t, acc):
+            if t == 0:
+                zs[b, h] = worked("zs", [P, PACK, NM], BF16, 2)
+            col = b * NH + h
+            nc.scalar.activation(out=zs[b, h][:, t, :], in_=acc[:], func=COPY, scale=kap_z[:, t, col : col + 1])
+
+        def groups(b, h, ts):
+            for t in ts:
                 acc = bank("acc", [P, NM], F32)
                 for g in range(NH):
-                    nc.tensor.matmul_mx(
-                        out=acc[:],
-                        lhsT=eta_st[h][:, t, g, :].bitcast(E2M1),
-                        lhsT_scale=scl_st[:, t, g, h, :],
-                        rhs=v_codes[b][:, g, :].bitcast(E4M3),
-                        rhs_scale=v_scl[b][:, g, :],
-                        start=(g == 0),
-                        stop=(g == NH - 1),
-                    )
-                col = b * NH + h
-                nc.scalar.activation(out=zs[:, t, :], in_=acc[:], func=COPY, scale=kap_z[:, t, col : col + 1])
-            return zs
+                    one_pass(b, h, t, g, acc)
+                fetch_z(b, h, t, acc)
 
-        def pack_z(zs):
-            zi = worked("zi", [P, NM, PACK], BF16, 2)
-            nc.vector.tensor_copy(out=zi[:], in_=zs[:].rearrange("p t n -> p n t"))
-            return zi
+        zi = {}
 
-        def quant_z(b, h, zi):
+        def pack_z(b, h):
+            zi[b, h] = worked("zi", [P, NM, PACK], BF16, 2)
+            nc.vector.tensor_copy(out=zi[b, h][:], in_=zs[b, h][:].rearrange("p t n -> p n t"))
+
+        def quant_z(b, h):
             nc.vector.quantize_mx(
-                out=z_codes[b][h][:].bitcast(E5M2), scales=z_scl[b][h][:], in_=zi[:].rearrange("p n t -> p (n t)")
+                out=z_codes[b][h][:].bitcast(E5M2), scales=z_scl[b][h][:], in_=zi[b, h][:].rearrange("p n t -> p (n t)")
             )
 
         def project(b, i, acc, hs):
@@ -238,85 +248,125 @@ def tile_photonic_rayleigh_gram_s9_kernel(tc, x, kappa, eta_words, eta_scales, y
                 nc.scalar.copy(out=res[:], in_=acc[:])
             nc.sync.dma_start(out=out[b, i * P : (i + 1) * P, :], in_=res[:])
 
-        units = [(q, g) for q in range(2) for g in range(NH)]
-        t0 = [turn_x(0, q, g, "tr") for q, g in units[:4]]
-        v0 = [scale_x_psum(0, units[0][1], t0[0])]
-        for n in range(1, 6):
-            if n + 3 < 6:
-                q, g = units[n + 3]
-                t0.append(turn_x(0, q, g, "tr"))
-            v0.append(scale_x_psum(0, units[n][1], t0[n]))
-            quant_x(0, units[n - 1][0], units[n - 1][1], v0[n - 1])
-            if n == 3:
-                permute_scales()
-            if n == 4:
-                permute_eta(0)
-        quant_x(0, units[5][0], units[5][1], v0[5])
-        xt1 = []
-        for n in range(6):
-            q, g = units[n]
-            xt1.append(fetch_x(turn_x(1, q, g, "acc" if n < 4 else "tr")))
+        units = [(q, g) for g in range(NH) for q in range(2)]
+        xb = {}
+        vs = {}
 
-        pending = []
+        def turn(b, *ns):
+            for n in ns:
+                xb[b, n] = turn_x(b, units[n][0], units[n][1], "tr")
 
-        def x1_step(n):
-            pending.append((n, scale_x(1, units[n][1], xt1[n])))
-            if len(pending) > 1:
-                x1_quant()
+        def mult(b, n):
+            vs[b, n] = scale_x_psum(b, units[n][1], xb[b, n])
 
-        def x1_quant():
-            n, v = pending.pop(0)
-            quant_x(1, units[n][0], units[n][1], v)
+        def quant(b, n):
+            quant_x(b, units[n][0], units[n][1], vs[b, n])
 
+        def early(g):
+            for t in range(PACK):
+                one_pass(0, 0, t, g, first[t])
+                if g == NH - 1:
+                    fetch_z(0, 0, t, first[t])
+
+        turn(0, 0)
+        spread_kappa()
+        turn(0, 1, 2, 3)
+        first = [bank("acc", [P, NM], F32) for t in range(PACK)]
+        permute_eta(0)
+        mult(0, 0)
+        mult(0, 1)
+        quant(0, 0)
+        quant(0, 1)
+        mult(0, 2)
+        permute_scales()
+        turn(0, 4)
+        early(0)
+        turn(0, 5)
+        mult(0, 3)
+        quant(0, 2)
+        quant(0, 3)
+        mult(0, 4)
+        early(1)
+        mult(0, 5)
+        quant(0, 4)
+        quant(0, 5)
+        turn(1, 0, 1)
+        reorder_y(0, 0, 0, False)
+        early(2)
         permute_eta(1)
-        zs00 = stage1(0, 0)
-        x1_step(0)
-        x1_step(1)
-        yo00 = reorder_y(0, 0)
-        zs01 = stage1(0, 1)
-        zi00 = pack_z(zs00)
-        x1_step(2)
-        quant_z(0, 0, zi00)
-        x1_step(3)
+        mult(1, 0)
+        mult(1, 1)
+        quant(1, 0)
+        quant(1, 1)
+        turn(1, 2, 3)
+        reorder_y(0, 0, 1, True)
+        reorder_y(0, 1, 0, False)
+        groups(0, 1, (0, 1))
+        mult(1, 2)
+        mult(1, 3)
+        quant(1, 2)
+        quant(1, 3)
+        turn(1, 4, 5)
+        reorder_y(0, 1, 1, False)
+        groups(0, 1, (2, 3))
+        pack_z(0, 0)
+        mult(1, 4)
+        quant_z(0, 0)
+        mult(1, 5)
         permute_eta(2)
-        yt00 = turn_y(yo00)
-        zs02 = stage1(0, 2)
-        zi01 = pack_z(zs01)
-        x1_step(4)
-        quant_z(0, 1, zi01)
-        x1_step(5)
-        x1_quant()
-        yo01 = reorder_y(0, 1)
-        quant_y(0, 0, yt00)
-        yt01 = turn_y(yo01)
-        zs10 = stage1(1, 0)
-        zi02 = pack_z(zs02)
-        yo10 = reorder_y(1, 0)
-        quant_z(0, 2, zi02)
-        quant_y(0, 1, yt01)
-        yt10 = turn_y(yo10)
-        zs11 = stage1(1, 1)
-        zi10 = pack_z(zs10)
-        yo11 = reorder_y(1, 1)
-        quant_z(1, 0, zi10)
-        quant_y(1, 0, yt10)
-        yt11 = turn_y(yo11)
-        zs12 = stage1(1, 2)
-        zi11 = pack_z(zs11)
-        quant_y(1, 1, yt11)
-        quant_z(1, 1, zi11)
+        quant(1, 4)
+        quant(1, 5)
+        reorder_y(1, 0, 0, True)
+        turn_y(0)
+        turn_y(1)
+        groups(0, 2, (0, 1))
+        pack_z(0, 1)
+        reorder_y(1, 0, 1, True)
+        quant_z(0, 1)
+        turn_y(2)
+        turn_y(3)
+        groups(0, 2, (2, 3))
+        quant_y(0)
+        quant_y(1)
+        reorder_y(1, 1, 0, True)
+        quant_y(2)
+        quant_y(3)
+        turn_y(4)
+        turn_y(5)
+        groups(1, 0, (0, 1))
+        pack_z(0, 2)
+        reorder_y(1, 1, 1, True)
+        quant_z(0, 2)
+        quant_y(4)
+        quant_y(5)
+        turn_y(6)
+        turn_y(7)
+        groups(1, 0, (2, 3))
+        quant_y(6)
+        quant_y(7)
+        turn_y(8)
+        turn_y(9)
+        groups(1, 1, (0, 1))
+        pack_z(1, 0)
+        quant_y(8)
+        quant_z(1, 0)
+        quant_y(9)
+        turn_y(10)
+        turn_y(11)
+        groups(1, 1, (2, 3))
+        quant_y(10)
+        quant_y(11)
+        groups(1, 2, range(PACK))
+        pack_z(1, 1)
+        quant_z(1, 1)
 
         for i in range(NM // P):
             acc = bank("tr", [P, NY], F32)
             project(0, i, acc, range(NH))
             store(0, i, acc, False)
-        zi12 = pack_z(zs12)
-        quant_z(1, 2, zi12)
-        accs = []
+        pack_z(1, 2)
+        quant_z(1, 2)
         for i in range(NM // P):
             acc = bank("acc", [P, NY], F32)
-            project(1, i, acc, range(NH - 1))
-            accs.append(acc)
-        for i in range(NM // P):
-            project(1, i, accs[i], [NH - 1])
-            store(1, i, accs[i], i % 2 == 1)
+            project(1, i, acc, range(NH))
+            store(1, i, acc, i % 2 == 1)

@@ -46,12 +46,12 @@ def tile_photonic_rayleigh_gram_s9_kernel(tc, x, kappa, eta_words, eta_scales, y
         scl_raw = kept("scl_raw", [P, NH, G], U8)
         kap_rows = kept("kap_rows", [P, K_PASS], BF16)
 
+        nc.vector.memset(kap_rows[:].bitcast(I32), 0)
         nc.vector.memset(scl_raw[:].rearrange("p g n -> p (g n)").bitcast(I32), 0)
-        nc.gpsimd.memset(kap_rows[:], 0.0)
-        ident_b = kept("ident_b", [P, P], BF16)
         ident_f = kept("ident_f", [P, P], F32)
-        make_identity(nc, ident_b[:])
+        ident_b = kept("ident_b", [P, P], BF16)
         make_identity(nc, ident_f[:])
+        make_identity(nc, ident_b[:])
 
         def rows_of(src, b, q):
             return src[b, 2 * P * q : 2 * P * (q + 1), :].rearrange("(a p) k -> p a k", p=P)
@@ -69,13 +69,13 @@ def tile_photonic_rayleigh_gram_s9_kernel(tc, x, kappa, eta_words, eta_scales, y
             )
 
         load_x(0, 0, 2, 0, 1)
+        nc.sync.dma_start(out=kap_rows[0 : NB * NH, :], in_=kappa.rearrange("b (h k) -> (b h) k", h=NH))
         load_eta(0)
         load_x(0, 2, 4, 0, 1)
-        nc.scalar.dma_start(out=kap_rows[0 : NB * NH, :], in_=kappa.rearrange("b (h k) -> (b h) k", h=NH))
         load_x(0, 0, 4, 1, 2)
         load_x(0, 0, 4, 2, 3)
         for quad in range(4):
-            nc.scalar.dma_start(
+            nc.gpsimd.dma_start(
                 out=scl_raw[32 * quad : 32 * quad + 4, :, :].bitcast(I32),
                 in_=eta_scales[:, 4 * quad : 4 * quad + 4, :].rearrange("g r n -> r g n").bitcast(I32),
             )
@@ -96,15 +96,17 @@ def tile_photonic_rayleigh_gram_s9_kernel(tc, x, kappa, eta_words, eta_scales, y
         kap_x = kept("kap_x", [P, NB * NH, PACK], BF16)
         kap_z = kept("kap_z", [P, PACK, NB * NH], F32)
 
-        def spread_kappa():
-            kap_bank = bank("acc", [P, 8, P], BF16)
+        def spread_kap_x():
+            spread = bank("acc", [P, PACK, P], BF16)
             for t in range(PACK):
-                nc.tensor.transpose(kap_bank[:, t, :], kap_rows[:, t::PACK], ident_b[:])
-            nc.scalar.copy(out=kap_x[:], in_=kap_bank[:, 0:4, 0 : NB * NH].rearrange("p t b -> p b t"))
-            kap_bank2 = bank("acc", [P, 8, P], BF16)
+                nc.tensor.transpose(spread[:, t, :], kap_rows[:, t::PACK], ident_b[:])
+            nc.scalar.copy(out=kap_x[:], in_=spread[:, :, 0 : NB * NH].rearrange("p t b -> p b t"))
+
+        def spread_kap_z():
+            spread = bank("tr", [P, PACK, P], BF16)
             for t in range(PACK):
-                nc.tensor.transpose(kap_bank2[:, t, :], kap_perm[:, t * P : (t + 1) * P], ident_b[:])
-            nc.scalar.copy(out=kap_z[:], in_=kap_bank2[:, 0:4, 0 : NB * NH])
+                nc.tensor.transpose(spread[:, t, :], kap_perm[:, t * P : (t + 1) * P], ident_b[:])
+            nc.scalar.copy(out=kap_z[:], in_=spread[:, :, 0 : NB * NH])
 
         v_codes = [kept("v_codes%d" % b, [P, NH, NM], U32) for b in range(NB)]
         v_scl = [kept("v_scl%d" % b, [P, NH, NM], U8) for b in range(NB)]
@@ -127,12 +129,26 @@ def tile_photonic_rayleigh_gram_s9_kernel(tc, x, kappa, eta_words, eta_scales, y
                 in_=scl_raw[:].rearrange("p g n -> p (g n)").bitcast(I32).rearrange("p (b t w) -> p t b w", t=4, w=2),
             )
 
-        def turn_x(b, q, g, tag):
-            turned = bank(tag, [P, 2, 2 * P], F32)
+        def split_x(b, q, g):
+            xs = worked("xs", [P, 2, 2, P], F32, 6)
+            nc.scalar.copy(
+                out=xs[:],
+                in_=x_raw[b][:, 2 * q : 2 * q + 2, :]
+                .rearrange("p a k -> p (a k)")
+                .bitcast(F32)
+                .rearrange("p (a k m u) -> p k a u m", a=2, k=NH, u=2)[:, g, :, :, :],
+            )
+            return xs
+
+        def turn_x(b, q, g, xs):
+            turned = bank("tr", [P, 2, 2 * P], F32)
             for a in range(2):
-                words = x_raw[b][:, 2 * q + a, :].bitcast(F32)
                 for u in range(2):
-                    nc.tensor.transpose(turned[:, u, a * P : (a + 1) * P], words[:, 256 * g + u : 256 * (g + 1) : 2], ident_f[:])
+                    if xs is None:
+                        words = x_raw[b][:, 2 * q + a, :].bitcast(F32)[:, 256 * g + u : 256 * (g + 1) : 2]
+                    else:
+                        words = xs[:, a, u, :]
+                    nc.tensor.transpose(turned[:, u, a * P : (a + 1) * P], words, ident_f[:])
             return turned
 
         def kap_for(b, g):
@@ -249,18 +265,25 @@ def tile_photonic_rayleigh_gram_s9_kernel(tc, x, kappa, eta_words, eta_scales, y
             nc.sync.dma_start(out=out[b, i * P : (i + 1) * P, :], in_=res[:])
 
         units = [(q, g) for g in range(NH) for q in range(2)]
+        xs = {}
         xb = {}
         vs = {}
 
+        def split(b, *ns):
+            for n in ns:
+                xs[b, n] = split_x(b, units[n][0], units[n][1])
+
         def turn(b, *ns):
             for n in ns:
-                xb[b, n] = turn_x(b, units[n][0], units[n][1], "tr")
+                xb[b, n] = turn_x(b, units[n][0], units[n][1], xs.get((b, n)))
 
-        def mult(b, n):
-            vs[b, n] = scale_x_psum(b, units[n][1], xb[b, n])
+        def mult(b, *ns):
+            for n in ns:
+                vs[b, n] = scale_x_psum(b, units[n][1], xb[b, n])
 
-        def quant(b, n):
-            quant_x(b, units[n][0], units[n][1], vs[b, n])
+        def quant(b, *ns):
+            for n in ns:
+                quant_x(b, units[n][0], units[n][1], vs[b, n])
 
         def early(g):
             for t in range(PACK):
@@ -268,94 +291,79 @@ def tile_photonic_rayleigh_gram_s9_kernel(tc, x, kappa, eta_words, eta_scales, y
                 if g == NH - 1:
                     fetch_z(0, 0, t, first[t])
 
+        def ty(*ns):
+            for n in ns:
+                turn_y(n)
+
+        def qy(*ns):
+            for n in ns:
+                quant_y(n)
+
+        S, V = False, True
         turn(0, 0)
-        spread_kappa()
-        turn(0, 1, 2, 3)
+        spread_kap_x()
+        turn(0, 1)
+        split(0, 2, 3, 4, 5)
+        turn(0, 2, 3)
         first = [bank("acc", [P, NM], F32) for t in range(PACK)]
         permute_eta(0)
-        mult(0, 0)
-        mult(0, 1)
+        mult(0, 0, 1)
+        turn(0, 4, 5)
         quant(0, 0)
-        quant(0, 1)
-        mult(0, 2)
         permute_scales()
-        turn(0, 4)
+        quant(0, 1)
+        mult(0, 2, 3)
         early(0)
-        turn(0, 5)
-        mult(0, 3)
-        quant(0, 2)
-        quant(0, 3)
-        mult(0, 4)
-        early(1)
-        mult(0, 5)
-        quant(0, 4)
-        quant(0, 5)
+        quant(0, 2, 3)
+        mult(0, 4, 5)
+        split(1, 0, 2, 4, 1, 3, 5)
         turn(1, 0, 1)
-        reorder_y(0, 0, 0, False)
-        early(2)
+        early(1)
+        quant(0, 4, 5)
+        reorder_y(0, 0, 1, S)
         permute_eta(1)
-        mult(1, 0)
-        mult(1, 1)
-        quant(1, 0)
-        quant(1, 1)
-        turn(1, 2, 3)
-        reorder_y(0, 0, 1, True)
-        reorder_y(0, 1, 0, False)
-        groups(0, 1, (0, 1))
-        mult(1, 2)
-        mult(1, 3)
-        quant(1, 2)
-        quant(1, 3)
-        turn(1, 4, 5)
-        reorder_y(0, 1, 1, False)
-        groups(0, 1, (2, 3))
-        pack_z(0, 0)
-        mult(1, 4)
-        quant_z(0, 0)
-        mult(1, 5)
+        spread_kap_z()
+        early(2)
+        mult(1, 0, 1)
+        reorder_y(0, 0, 0, V)
+        quant(1, 0, 1)
         permute_eta(2)
-        quant(1, 4)
-        quant(1, 5)
-        reorder_y(1, 0, 0, True)
-        turn_y(0)
-        turn_y(1)
+        turn(1, 2, 3)
+        groups(0, 1, (0, 1))
+        mult(1, 2, 3)
+        quant(1, 2, 3)
+        pack_z(0, 0)
+        turn(1, 4, 5)
+        groups(0, 1, (2, 3))
+        quant_z(0, 0)
+        mult(1, 4, 5)
+        reorder_y(0, 1, 0, S)
+        quant(1, 4, 5)
+        reorder_y(0, 1, 1, V)
+        ty(0, 1, 2)
         groups(0, 2, (0, 1))
         pack_z(0, 1)
-        reorder_y(1, 0, 1, True)
+        qy(0, 1, 2)
         quant_z(0, 1)
-        turn_y(2)
-        turn_y(3)
+        reorder_y(1, 0, 1, V)
+        ty(3, 4, 5)
         groups(0, 2, (2, 3))
-        quant_y(0)
-        quant_y(1)
-        reorder_y(1, 1, 0, True)
-        quant_y(2)
-        quant_y(3)
-        turn_y(4)
-        turn_y(5)
+        reorder_y(1, 0, 0, V)
+        qy(3, 4, 5)
         groups(1, 0, (0, 1))
         pack_z(0, 2)
-        reorder_y(1, 1, 1, True)
+        reorder_y(1, 1, 0, V)
         quant_z(0, 2)
-        quant_y(4)
-        quant_y(5)
-        turn_y(6)
-        turn_y(7)
+        ty(6, 7, 8)
         groups(1, 0, (2, 3))
-        quant_y(6)
-        quant_y(7)
-        turn_y(8)
-        turn_y(9)
+        reorder_y(1, 1, 1, V)
+        qy(6, 7, 8)
         groups(1, 1, (0, 1))
         pack_z(1, 0)
-        quant_y(8)
+        ty(9, 10, 11)
         quant_z(1, 0)
-        quant_y(9)
-        turn_y(10)
-        turn_y(11)
         groups(1, 1, (2, 3))
-        quant_y(10)
-        quant_y(11)
+        qy(9, 10, 11)
         groups(1, 2, range(PACK))
         pack_z(1, 1)
         quant_z(1, 1)
@@ -369,4 +377,4 @@ def tile_photonic_rayleigh_gram_s9_kernel(tc, x, kappa, eta_words, eta_scales, y
         for i in range(NM // P):
             acc = bank("acc", [P, NY], F32)
             project(1, i, acc, range(NH))
-            store(1, i, acc, i % 2 == 1)
+            store(1, i, acc, False)

@@ -40,7 +40,7 @@ def tile_photonic_rayleigh_gram_s9_kernel(tc, x, kappa, eta_words, eta_scales, y
         def bank(tag, shape, dtype):
             return psum.tile(shape, dtype, name="bank_" + tag, tag=tag, bufs=4)
 
-        x_raw = [kept("x_raw%d" % b, [P, NM // P, G], BF16) for b in range(NB)]
+        x_raw = [kept("x_raw%d" % b, [P, NH, NM // P, K_PASS], BF16) for b in range(NB)]
         y_raw = [[kept("y_raw%d%d" % (b, q), [P, 2, G], BF16) for q in range(2)] for b in range(NB)]
         eta_raw = [kept("eta_raw%d" % h, [P, NH, 2 * K_PASS], U8) for h in range(NH)]
         scl_raw = kept("scl_raw", [P, NH, G], U8)
@@ -62,25 +62,25 @@ def tile_photonic_rayleigh_gram_s9_kernel(tc, x, kappa, eta_words, eta_scales, y
                 in_=eta_words[:, :, 2 * K_PASS * h : 2 * K_PASS * (h + 1)].rearrange("g p n -> p g n"),
             )
 
-        def load_x(b, a0, a1, g0, g1):
+        def load_x(b, g, a0, a1):
             nc.sync.dma_start(
-                out=x_raw[b][:, a0:a1, g0 * K_PASS : g1 * K_PASS],
-                in_=x[b, a0 * P : a1 * P, g0 * K_PASS : g1 * K_PASS].rearrange("(a p) k -> p a k", p=P),
+                out=x_raw[b][:, g, a0:a1, :],
+                in_=x[b, a0 * P : a1 * P, g * K_PASS : (g + 1) * K_PASS].rearrange("(a p) k -> p a k", p=P),
             )
 
-        load_x(0, 0, 2, 0, 1)
+        load_x(0, 0, 0, 2)
         nc.sync.dma_start(out=kap_rows[0 : NB * NH, :], in_=kappa.rearrange("b (h k) -> (b h) k", h=NH))
         load_eta(0)
-        load_x(0, 2, 4, 0, 1)
-        load_x(0, 0, 4, 1, 2)
-        load_x(0, 0, 4, 2, 3)
+        load_x(0, 0, 2, 4)
+        load_x(0, 1, 0, 4)
+        load_x(0, 2, 0, 4)
         for quad in range(4):
-            nc.gpsimd.dma_start(
+            nc.sync.dma_start(
                 out=scl_raw[32 * quad : 32 * quad + 4, :, :].bitcast(I32),
                 in_=eta_scales[:, 4 * quad : 4 * quad + 4, :].rearrange("g r n -> r g n").bitcast(I32),
             )
-        load_x(1, 0, 2, 0, NH)
-        load_x(1, 2, 4, 0, NH)
+        for g in range(NH):
+            load_x(1, g, 0, 4)
         load_eta(1)
         nc.sync.dma_start(out=y_raw[0][0][:], in_=rows_of(y, 0, 0))
         load_eta(2)
@@ -133,10 +133,10 @@ def tile_photonic_rayleigh_gram_s9_kernel(tc, x, kappa, eta_words, eta_scales, y
             xs = worked("xs", [P, 2, 2, P], F32, 6)
             nc.scalar.copy(
                 out=xs[:],
-                in_=x_raw[b][:, 2 * q : 2 * q + 2, :]
+                in_=x_raw[b][:, g, 2 * q : 2 * q + 2, :]
                 .rearrange("p a k -> p (a k)")
                 .bitcast(F32)
-                .rearrange("p (a k m u) -> p k a u m", a=2, k=NH, u=2)[:, g, :, :, :],
+                .rearrange("p (a m u) -> p a u m", a=2, u=2),
             )
             return xs
 
@@ -145,7 +145,7 @@ def tile_photonic_rayleigh_gram_s9_kernel(tc, x, kappa, eta_words, eta_scales, y
             for a in range(2):
                 for u in range(2):
                     if xs is None:
-                        words = x_raw[b][:, 2 * q + a, :].bitcast(F32)[:, 256 * g + u : 256 * (g + 1) : 2]
+                        words = x_raw[b][:, g, 2 * q + a, :].bitcast(F32)[:, u::2]
                     else:
                         words = xs[:, a, u, :]
                     nc.tensor.transpose(turned[:, u, a * P : (a + 1) * P], words, ident_f[:])
@@ -237,7 +237,10 @@ def tile_photonic_rayleigh_gram_s9_kernel(tc, x, kappa, eta_words, eta_scales, y
 
         def pack_z(b, h):
             zi[b, h] = worked("zi", [P, NM, PACK], BF16, 2)
-            nc.vector.tensor_copy(out=zi[b, h][:], in_=zs[b, h][:].rearrange("p t n -> p n t"))
+            nc.vector.tensor_copy(
+                out=zi[b, h][:].rearrange("p (c i) t -> p c t i", i=4),
+                in_=zs[b, h][:].rearrange("p t (c i) -> p c t i", i=4),
+            )
 
         def quant_z(b, h):
             nc.vector.quantize_mx(
@@ -310,20 +313,20 @@ def tile_photonic_rayleigh_gram_s9_kernel(tc, x, kappa, eta_words, eta_scales, y
         mult(0, 0, 1)
         turn(0, 4, 5)
         quant(0, 0)
-        permute_scales()
         quant(0, 1)
         mult(0, 2, 3)
+        permute_scales()
         early(0)
         quant(0, 2, 3)
         mult(0, 4, 5)
-        split(1, 0, 2, 4, 1, 3, 5)
+        split(1, 0, 1, 2, 3, 4, 5)
         turn(1, 0, 1)
+        spread_kap_z()
         early(1)
         quant(0, 4, 5)
-        reorder_y(0, 0, 1, S)
         permute_eta(1)
-        spread_kap_z()
         early(2)
+        reorder_y(0, 0, 1, S)
         mult(1, 0, 1)
         reorder_y(0, 0, 0, V)
         quant(1, 0, 1)

from contextlib import ExitStack

import concourse.mybir as mybir
from concourse.masks import make_identity

NB, NM, NY, G = 2, 512, 512, 1536
P = 128
K_PASS = 512
NH = G // K_PASS
PACK = 4

F32 = mybir.dt.float32
BF16 = mybir.dt.bfloat16
I32 = mybir.dt.int32
U32 = mybir.dt.uint32
U8 = mybir.dt.uint8
E4M3 = mybir.dt.float8_e4m3fn_x4
E5M2 = mybir.dt.float8_e5m2_x4
E2M1 = mybir.dt.float4_e2m1fn_x4
MULT = mybir.AluOpType.mult
COPY = mybir.ActivationFunctionType.Copy

FLOPS = 2 * NB * NM * G * (G + NY)


def tile_photonic_rayleigh_gram_s9_kernel(tc, x, kappa, eta_words, eta_scales, y, out):
    nc = tc.nc
    with ExitStack() as ctx:
        ctx.enter_context(tc.manual_schedule())
        keep = ctx.enter_context(tc.tile_pool(name="keep", bufs=1))
        work = ctx.enter_context(tc.tile_pool(name="work", bufs=2))
        psum = ctx.enter_context(tc.psum_pool(name="psum", bufs=4))

        def kept(name, shape, dtype):
            return keep.tile(shape, dtype, name=name, tag=name, align_bytes=64)

        def worked(name, shape, dtype, bufs):
            return work.tile(shape, dtype, name=name, tag=name, bufs=bufs, align_bytes=64)

        def bank(tag, shape, dtype):
            return psum.tile(shape, dtype, name="bank_" + tag, tag=tag, bufs=4)

        x_raw = [kept("x_raw%d" % b, [P, NH, NM // P, K_PASS], BF16) for b in range(NB)]
        y_raw = [[kept("y_raw%d%d" % (b, q), [P, 2, G], BF16) for q in range(2)] for b in range(NB)]
        eta_raw = [kept("eta_raw%d" % h, [P, NH, 2 * K_PASS], U8) for h in range(NH)]
        scl_raw = kept("scl_raw", [P, NH, G], U8)
        kap_rows = kept("kap_rows", [P, K_PASS], BF16)

        nc.vector.memset(kap_rows[:].bitcast(I32), 0)
        nc.vector.memset(scl_raw[:].rearrange("p g n -> p (g n)").bitcast(I32), 0)
        ident_f = kept("ident_f", [P, P], F32)
        ident_b = kept("ident_b", [P, P], BF16)
        make_identity(nc, ident_f[:])
        make_identity(nc, ident_b[:])

        def rows_of(src, b, q):
            return src[b, 2 * P * q : 2 * P * (q + 1), :].rearrange("(a p) k -> p a k", p=P)

        def load_eta(h):
            nc.sync.dma_start(
                out=eta_raw[h][:],
                in_=eta_words[:, :, 2 * K_PASS * h : 2 * K_PASS * (h + 1)].rearrange("g p n -> p g n"),
            )

        def load_x(b, g, a0, a1):
            nc.sync.dma_start(
                out=x_raw[b][:, g, a0:a1, :],
                in_=x[b, a0 * P : a1 * P, g * K_PASS : (g + 1) * K_PASS].rearrange("(a p) k -> p a k", p=P),
            )

        load_x(0, 0, 0, 2)
        nc.sync.dma_start(out=kap_rows[0 : NB * NH, :], in_=kappa.rearrange("b (h k) -> (b h) k", h=NH))
        load_eta(0)
        load_x(0, 0, 2, 4)
        load_x(0, 1, 0, 4)
        load_x(0, 2, 0, 4)
        for quad in range(4):
            nc.sync.dma_start(
                out=scl_raw[32 * quad : 32 * quad + 4, :, :].bitcast(I32),
                in_=eta_scales[:, 4 * quad : 4 * quad + 4, :].rearrange("g r n -> r g n").bitcast(I32),
            )
        for g in range(NH):
            load_x(1, g, 0, 4)
        load_eta(1)
        nc.sync.dma_start(out=y_raw[0][0][:], in_=rows_of(y, 0, 0))
        load_eta(2)
        nc.sync.dma_start(out=y_raw[0][1][:], in_=rows_of(y, 0, 1))
        nc.sync.dma_start(out=y_raw[1][0][:], in_=rows_of(y, 1, 0))
        nc.sync.dma_start(out=y_raw[1][1][:], in_=rows_of(y, 1, 1))

        kap_perm = kept("kap_perm", [P, K_PASS], BF16)
        nc.vector.tensor_copy(
            out=kap_perm[:].rearrange("p (t b m) -> p t b m", t=4, m=8),
            in_=kap_rows[:].rearrange("p (b t m) -> p t b m", t=4, m=8),
        )
        kap_x = kept("kap_x", [P, NB * NH, PACK], BF16)
        kap_z = kept("kap_z", [P, PACK, NB * NH], F32)

        def spread_kap_x():
            spread = bank("acc", [P, PACK, P], BF16)
            for t in range(PACK):
                nc.tensor.transpose(spread[:, t, :], kap_rows[:, t::PACK], ident_b[:])
            nc.scalar.copy(out=kap_x[:], in_=spread[:, :, 0 : NB * NH].rearrange("p t b -> p b t"))

        def spread_kap_z():
            spread = bank("tr", [P, PACK, P], BF16)
            for t in range(PACK):
                nc.tensor.transpose(spread[:, t, :], kap_perm[:, t * P : (t + 1) * P], ident_b[:])
            nc.scalar.copy(out=kap_z[:], in_=spread[:, :, 0 : NB * NH])

        v_codes = [kept("v_codes%d" % b, [P, NH, NM], U32) for b in range(NB)]
        v_scl = [kept("v_scl%d" % b, [P, NH, NM], U8) for b in range(NB)]
        y_codes = [kept("y_codes%d" % b, [P, NH, NY], U32) for b in range(NB)]
        y_scl = [kept("y_scl%d" % b, [P, NH, NY], U8) for b in range(NB)]
        z_codes = [[kept("z_codes%d%d" % (b, h), [P, NM], U32) for h in range(NH)] for b in range(NB)]
        z_scl = [[kept("z_scl%d%d" % (b, h), [P, NM], U8) for h in range(NH)] for b in range(NB)]
        eta_st = [kept("eta_st%d" % h, [P, PACK, NH, 2 * P], U8) for h in range(NH)]
        scl_st = kept("scl_st", [P, PACK, NH, NH, P], U8)

        def permute_eta(h):
            nc.vector.tensor_copy(
                out=eta_st[h][:].rearrange("p t g n -> p (t g n)").bitcast(I32).rearrange("p (t b w) -> p t b w", t=4, w=4),
                in_=eta_raw[h][:].rearrange("p g n -> p (g n)").bitcast(I32).rearrange("p (b t w) -> p t b w", t=4, w=4),
            )

        def permute_scales():
            nc.vector.tensor_copy(
                out=scl_st[:].rearrange("p t g h n -> p (t g h n)").bitcast(I32).rearrange("p (t b w) -> p t b w", t=4, w=2),
                in_=scl_raw[:].rearrange("p g n -> p (g n)").bitcast(I32).rearrange("p (b t w) -> p t b w", t=4, w=2),
            )

        def split_x(b, q, g):
            xs = worked("xs", [P, 2, 2, P], F32, 6)
            nc.scalar.copy(
                out=xs[:],
                in_=x_raw[b][:, g, 2 * q : 2 * q + 2, :]
                .rearrange("p a k -> p (a k)")
                .bitcast(F32)
                .rearrange("p (a m u) -> p a u m", a=2, u=2),
            )
            return xs

        def turn_x(b, q, g, xs):
            turned = bank("tr", [P, 2, 2 * P], F32)
            for a in range(2):
                for u in range(2):
                    if xs is None:
                        words = x_raw[b][:, g, 2 * q + a, :].bitcast(F32)[:, u::2]
                    else:
                        words = xs[:, a, u, :]
                    nc.tensor.transpose(turned[:, u, a * P : (a + 1) * P], words, ident_f[:])
            return turned

        def kap_for(b, g):
            row = kap_x[:, b * NH + g, :].unsqueeze(1).to_broadcast([P, 2 * P, PACK])
            return row

        def scale_x_psum(b, g, turned):
            v = worked("v", [P, 2 * P, PACK], BF16, 4)
            nc.vector.tensor_tensor(
                out=v[:].rearrange("p r (u e) -> p r u e", e=2),
                in0=turned[:].rearrange("p u r -> p (u r)").bitcast(BF16).rearrange("p (u r e) -> p r u e", u=2, e=2),
                in1=kap_for(b, g).rearrange("p r (u e) -> p r u e", e=2),
                op=MULT,
            )
            return v

        def quant_x(b, q, g, v):
            cols = slice(2 * P * q, 2 * P * (q + 1))
            nc.vector.quantize_mx(
                out=v_codes[b][:, g, cols].bitcast(E4M3), scales=v_scl[b][:, g, cols], in_=v[:].rearrange("p r t -> p (r t)")
            )

        yo = {}

        def reorder_y(b, q, a, on_vector):
            if (b, q) not in yo:
                yo[b, q] = worked("yo", [P, 2, 2, G // 2], BF16, 4)
            dst = yo[b, q][:, a, :, :].rearrange("p s (b m e) -> p s b m e", m=8, e=2)
            src = y_raw[b][q][:, a, :].rearrange("p (b s e m) -> p s b m e", s=2, e=2, m=8)
            if on_vector:
                nc.vector.tensor_copy(out=dst, in_=src)
            else:
                nc.scalar.copy(out=dst, in_=src)

        yt = {}

        def turn_y(n):
            b, q, h = n // 6, n // 3 % 2, n % 3
            turned = bank("tr", [P, 2, 2 * P], F32)
            for a in range(2):
                for s in range(2):
                    words = yo[b, q][:, a, s, :].bitcast(F32)
                    nc.tensor.transpose(turned[:, s, a * P : (a + 1) * P], words[:, h * P : (h + 1) * P], ident_f[:])
            yt[n] = worked("yt", [P, 2 * P, PACK], BF16, 4)
            nc.scalar.copy(
                out=yt[n][:].rearrange("p r t -> p (r t)").bitcast(F32).rearrange("p (r s) -> p r s", s=2),
                in_=turned[:].rearrange("p s r -> p r s"),
            )

        def quant_y(n):
            b, q, h = n // 6, n // 3 % 2, n % 3
            cols = slice(2 * P * q, 2 * P * (q + 1))
            nc.vector.quantize_mx(
                out=y_codes[b][:, h, cols].bitcast(E4M3),
                scales=y_scl[b][:, h, cols],
                in_=yt[n][:].rearrange("p r t -> p (r t)"),
            )

        def one_pass(b, h, t, g, acc):
            nc.tensor.matmul_mx(
                out=acc[:],
                lhsT=eta_st[h][:, t, g, :].bitcast(E2M1),
                lhsT_scale=scl_st[:, t, g, h, :],
                rhs=v_codes[b][:, g, :].bitcast(E4M3),
                rhs_scale=v_scl[b][:, g, :],
                start=(g == 0),
                stop=(g == NH - 1),
            )

        zs = {}

        def fetch_z(b, h, t, acc):
            if t == 0:
                zs[b, h] = worked("zs", [P, PACK, NM], BF16, 2)
            col = b * NH + h
            nc.scalar.activation(out=zs[b, h][:, t, :], in_=acc[:], func=COPY, scale=kap_z[:, t, col : col + 1])

        def groups(b, h, ts):
            for t in ts:
                acc = bank("acc", [P, NM], F32)
                for g in range(NH):
                    one_pass(b, h, t, g, acc)
                fetch_z(b, h, t, acc)

        zi = {}

        def pack_z(b, h):
            zi[b, h] = worked("zi", [P, NM, PACK], BF16, 2)
            nc.vector.tensor_copy(
                out=zi[b, h][:].rearrange("p (c i) t -> p c t i", i=4),
                in_=zs[b, h][:].rearrange("p t (c i) -> p c t i", i=4),
            )

        def quant_z(b, h):
            nc.vector.quantize_mx(
                out=z_codes[b][h][:].bitcast(E5M2), scales=z_scl[b][h][:], in_=zi[b, h][:].rearrange("p n t -> p (n t)")
            )

        def project(b, i, acc, hs):
            for h in hs:
                nc.tensor.matmul_mx(
                    out=acc[:],
                    lhsT=z_codes[b][h][:, i * P : (i + 1) * P].bitcast(E5M2),
                    lhsT_scale=z_scl[b][h][:, i * P : (i + 1) * P],
                    rhs=y_codes[b][:, h, :].bitcast(E4M3),
                    rhs_scale=y_scl[b][:, h, :],
                    start=(h == 0),
                    stop=(h == NH - 1),
                )

        def store(b, i, acc, on_vector):
            res = worked("res", [P, NY], F32, 8)
            if on_vector:
                nc.vector.tensor_copy(out=res[:], in_=acc[:])
            else:
                nc.scalar.copy(out=res[:], in_=acc[:])
            nc.sync.dma_start(out=out[b, i * P : (i + 1) * P, :], in_=res[:])

        units = [(q, g) for g in range(NH) for q in range(2)]
        xs = {}
        xb = {}
        vs = {}

        def split(b, *ns):
            for n in ns:
                xs[b, n] = split_x(b, units[n][0], units[n][1])

        def turn(b, *ns):
            for n in ns:
                xb[b, n] = turn_x(b, units[n][0], units[n][1], xs.get((b, n)))

        def mult(b, *ns):
            for n in ns:
                vs[b, n] = scale_x_psum(b, units[n][1], xb[b, n])

        def quant(b, *ns):
            for n in ns:
                quant_x(b, units[n][0], units[n][1], vs[b, n])

        def early(g):
            for t in range(PACK):
                one_pass(0, 0, t, g, first[t])
                if g == NH - 1:
                    fetch_z(0, 0, t, first[t])

        def ty(*ns):
            for n in ns:
                turn_y(n)

        def qy(*ns):
            for n in ns:
                quant_y(n)

        S, V = False, True
        turn(0, 0)
        spread_kap_x()
        turn(0, 1)
        split(0, 2, 3, 4, 5)
        turn(0, 2, 3)
        first = [bank("acc", [P, NM], F32) for t in range(PACK)]
        permute_eta(0)
        mult(0, 0, 1)
        turn(0, 4, 5)
        quant(0, 0)
        quant(0, 1)
        mult(0, 2, 3)
        permute_scales()
        early(0)
        quant(0, 2, 3)
        mult(0, 4, 5)
        split(1, 0, 1, 2, 3, 4, 5)
        turn(1, 0, 1)
        spread_kap_z()
        early(1)
        quant(0, 4, 5)
        permute_eta(1)
        early(2)
        reorder_y(0, 0, 1, S)
        mult(1, 0, 1)
        reorder_y(0, 0, 0, V)
        quant(1, 0, 1)
        permute_eta(2)
        turn(1, 2, 3)
        groups(0, 1, (0, 1))
        mult(1, 2, 3)
        quant(1, 2, 3)
        pack_z(0, 0)
        turn(1, 4, 5)
        groups(0, 1, (2, 3))
        quant_z(0, 0)
        mult(1, 4, 5)
        reorder_y(0, 1, 0, S)
        quant(1, 4, 5)
        reorder_y(0, 1, 1, V)
        ty(0, 1, 2)
        groups(0, 2, (0, 1))
        pack_z(0, 1)
        qy(0, 1, 2)
        quant_z(0, 1)
        reorder_y(1, 0, 1, V)
        ty(3, 4, 5)
        groups(0, 2, (2, 3))
        reorder_y(1, 0, 0, V)
        qy(3, 4, 5)
        groups(1, 0, (0, 1))
        pack_z(0, 2)
        reorder_y(1, 1, 0, V)
        quant_z(0, 2)
        ty(6, 7, 8)
        groups(1, 0, (2, 3))
        reorder_y(1, 1, 1, V)
        qy(6, 7, 8)
        groups(1, 1, (0, 1))
        pack_z(1, 0)
        ty(9, 10, 11)
        quant_z(1, 0)
        groups(1, 1, (2, 3))
        qy(9, 10, 11)
        groups(1, 2, range(PACK))
        pack_z(1, 1)
        quant_z(1, 1)

        for i in range(NM // P):
            acc = bank("tr", [P, NY], F32)
            project(0, i, acc, range(NH))
            store(0, i, acc, False)
        pack_z(1, 2)
        quant_z(1, 2)
        for i in range(NM // P):
            acc = bank("acc", [P, NY], F32)
            project(1, i, acc, range(NH))
            store(1, i, acc, False)
